import numpy as np
import ml_dtypes


def mxq(x, axis, fmt="e4m3"):
    dtype, down = {"e4m3": (ml_dtypes.float8_e4m3fn, 7), "e5m2": (ml_dtypes.float8_e5m2, 14)}[fmt]
    v = np.moveaxis(np.asarray(x, np.float32).astype(ml_dtypes.bfloat16).astype(np.float64), axis, -1)
    blocks = v.reshape(v.shape[:-1] + (-1, 32))
    amax = np.abs(blocks).max(-1, keepdims=True)
    byte = np.maximum(np.where(amax > 0, np.frexp(amax)[1] - 1 + 127, 0) - down, 1)
    scale = np.exp2(byte - 127.0)
    codes = (blocks / scale).astype(np.float32).astype(dtype).astype(np.float64)
    return np.moveaxis((codes * scale).reshape(v.shape), -1, axis)


WIDE = False


def mx_kscale(k):
    if not WIDE:
        return np.ones(k)
    levels = np.array([10, -10, 5, -5, 0])
    if k % 512:
        return np.exp2(np.random.permutation(np.resize(levels, k // 32))).repeat(32)
    a = np.empty((k // 512, 16))
    for p in range(k // 512):
        a[p, :8] = np.random.permutation(np.resize(levels, 8))
        for g in range(8):
            far = levels[np.abs(levels - a[p, g]) >= 10]
            a[p, g + 8] = far[np.random.randint(len(far))]
    return np.exp2(a.ravel()).repeat(32)


def f64(x):
    return np.asarray(x).astype(np.float64)


def striped(idx):
    return np.tile(idx.reshape(-1, 16).T, (8, 1)).astype(np.uint16)


def unstriped(offs):
    return offs[:16].T.reshape(-1).astype(np.int64)

def planes(y):
    n, m = y.shape
    v = y.astype(np.float32).astype(ml_dtypes.bfloat16).astype(np.float64).reshape(n // 32, 32, m)
    top = np.abs(v).max(1)
    byte = np.clip(np.where(top > 0, np.frexp(top)[1] - 1 + 127 - 7, 1), 1, 254)
    codes = (v * np.exp2(127.0 - byte)[:, None, :]).reshape(n, m).astype(np.float32).astype(ml_dtypes.float8_e4m3fn).view(np.uint8)
    words = codes.reshape(n // 512, 128, 4, m).transpose(0, 1, 3, 2)
    return np.ascontiguousarray(words), np.ascontiguousarray(byte.astype(np.uint8).reshape(n // 512, 16, m))


K, T, S, N, U = 512, 1024, 512, 512, 1024
P = 2 ** 7


def setup_inputs():
    n = np.random.standard_normal
    s = mx_kscale(K)[:, None]
    return {
        "xT": (n((K, T)) * s).astype(np.float32),
        "gate": np.tile(np.random.uniform(0.5, 1.5, S), (P, 1)).astype(np.float32),
        "w1": (n((K, N)) / np.sqrt(K) / s).astype(np.float32),
        "offs": striped(np.random.permutation(T)[:S]),
        "dst": striped(np.random.permutation(U)[:S]),
    }


def reference(xT, gate, w1, offs, dst):
    xq = mxq(f64(xT)[:, unstriped(offs)], 0, "e4m3")
    y = mxq(f64(w1), 0, "e4m3").T @ xq
    out = np.zeros((N, U))
    out[:, unstriped(dst)] = y * f64(gate)[:1]
    return (out,) + planes(out)

@@ -1,0 +1,180 @@
+from contextlib import ExitStack
+
+import concourse.mybir as mybir
+from concourse.masks import make_identity
+
+K, T, S, N, U = 512, 1024, 512, 512, 1024
+FLOPS = 2 * K * N * S
+
+F32 = mybir.dt.float32
+BF16 = mybir.dt.bfloat16
+I32 = mybir.dt.int32
+U32 = mybir.dt.uint32
+U16 = mybir.dt.uint16
+U8 = mybir.dt.uint8
+FP8X4 = mybir.dt.float8_e4m3fn_x4
+MULT = mybir.AluOpType.mult
+
+P = 128
+PACK = 4
+HALF = S // 2
+LIST_COLS = S // 16
+GROUPS = N // P
+QUARTER = U // 4
+
+
+def weave(engine_copy, out, in_):
+    engine_copy(
+        out.rearrange("p (c i) t -> p c t i", i=4),
+        in_.rearrange("p t (c i) -> p c t i", i=4),
+    )
+
+
+def quantize(nc, codes, scales, woven):
+    nc.vector.quantize_mx(out=codes.bitcast(FP8X4), scales=scales, in_=woven.rearrange("p c t -> p (c t)"))
+
+
+def tile_picked_route2_linnone_lo_kernel(
+    tc, xT, gate, w1, offs, dst, out_0, out_1, out_2
+):
+    nc = tc.nc
+    x_rows = xT.rearrange("(p j) t -> p j t", j=PACK)
+    w_rows = w1.rearrange("(p j) n -> p j n", j=PACK)
+    words_hbm = out_1[0].rearrange("l c r -> l (c r)").bitcast(I32).rearrange("(g l) (q c) -> q l g c", g=GROUPS, q=4)
+    scales_hbm = out_2[0].bitcast(I32).rearrange("(g b) (q c) -> q b g c", g=GROUPS, q=4)
+
+    with ExitStack() as ctx:
+        sb = ctx.enter_context(tc.tile_pool(name="sb", bufs=1))
+        ring = ctx.enter_context(tc.tile_pool(name="ring", bufs=4))
+        ps = ctx.enter_context(tc.psum_pool(name="ps", bufs=1))
+
+        offs_sb = sb.tile([P, LIST_COLS], U16, name="offs_sb")
+        dst_sb = sb.tile([P, LIST_COLS], U16, name="dst_sb")
+        x_sb = [sb.tile([P, T], F32, name="x%d" % j) for j in range(PACK)]
+        w_first = [sb.tile([P, PACK, P], F32, name="w%d" % g) for g in range(2)]
+        w_late = sb.tile([P, PACK, 2 * P], F32, name="w_late", tag="late")
+        gate_sb = sb.tile([P, S], F32, name="gate_sb")
+
+        nc.sync.dma_start(offs_sb[:], offs)
+        for j in range(PACK - 1):
+            nc.sync.dma_start(x_sb[j][:], x_rows[:, j, :])
+        nc.sync.dma_start(w_first[0][:], w_rows[:, :, 0:P])
+        nc.sync.dma_start(x_sb[PACK - 1][:], x_rows[:, PACK - 1, :])
+        nc.sync.dma_start(w_first[1][:], w_rows[:, :, P : 2 * P])
+        nc.sync.dma_start(gate_sb[:], gate)
+        nc.sync.dma_start(dst_sb[:], dst)
+        nc.sync.dma_start(w_late[:], w_rows[:, :, 2 * P :])
+
+        windows = [sb.tile([P, U], F32, name="window%d" % g) for g in range(GROUPS)]
+        nc.vector.memset(windows[0][:], 0.0)
+        ident = sb.tile([P, P], F32, name="ident")
+        make_identity(nc, ident[:])
+        for g in range(1, GROUPS):
+            nc.gpsimd.memset(windows[g][:], 0.0)
+
+        def list_half(list_sb, a):
+            return list_sb[:, a * LIST_COLS // 2 : (a + 1) * LIST_COLS // 2]
+
+        picked01 = [sb.tile([P, 2, HALF], F32, name="picked01_%d" % a) for a in range(2)]
+        x_woven = [sb.tile([P, HALF, PACK], BF16, name="x_woven%d" % a, align_bytes=64) for a in range(2)]
+        for j in range(2):
+            for a in range(2):
+                nc.vector.tensor_copy(picked01[a][:, j, :], x_sb[j][:].indirect(list_half(offs_sb, a)))
+        for a in range(2):
+            weave(nc.scalar.copy, x_woven[a][:, :, 0:2], picked01[a][:])
+
+        def gather_woven(j, a):
+            nc.vector.tensor_copy(x_woven[a][:, :, j], x_sb[j][:].indirect(list_half(offs_sb, a)))
+
+        x_codes = sb.tile([P, S], U32, name="x_codes", align_bytes=64)
+        x_scales = sb.tile([P, S], U8, name="x_scales", align_bytes=64)
+        widths = [P, P, 2 * P]
+        w_woven = [sb.tile([P, n, PACK], BF16, name="w_woven%d" % i, align_bytes=64) for i, n in enumerate(widths)]
+        w_codes = [sb.tile([P, n], U32, name="w_codes%d" % i, align_bytes=64) for i, n in enumerate(widths)]
+        w_scales = [sb.tile([P, n], U8, name="w_scales%d" % i, align_bytes=64) for i, n in enumerate(widths)]
+
+        def product(piece, w_cols, entries, y, bank):
+            acc = ps.tile([P, S], F32, name="acc", tag=bank)
+            n = entries.stop - entries.start
+            nc.tensor.matmul_mx(
+                out=acc[:, 0:n],
+                lhsT=w_codes[piece][:, w_cols].bitcast(FP8X4),
+                lhsT_scale=w_scales[piece][:, w_cols],
+                rhs=x_codes[:, entries].bitcast(FP8X4),
+                rhs_scale=x_scales[:, entries],
+                start=True,
+                stop=True,
+            )
+            nc.scalar.copy(y, acc[:, 0:n])
+
+        halves = [slice(0, HALF), slice(HALF, S)]
+        gather_woven(2, 0)
+        gather_woven(2, 1)
+        weave(nc.scalar.copy, w_woven[0][:], w_first[0][:])
+        gather_woven(3, 0)
+        quantize(nc, w_codes[0][:], w_scales[0][:], w_woven[0][:])
+        quantize(nc, x_codes[:, halves[0]], x_scales[:, halves[0]], x_woven[0][:])
+        gather_woven(3, 1)
+        quantize(nc, x_codes[:, halves[1]], x_scales[:, halves[1]], x_woven[1][:])
+        y_first = [sb.tile([P, HALF], F32, name="y_first%d" % a) for a in range(2)]
+        product(0, slice(0, P), halves[0], y_first[0][:], "turned10")
+        weave(nc.scalar.copy, w_woven[1][:], w_first[1][:])
+        quantize(nc, w_codes[1][:], w_scales[1][:], w_woven[1][:])
+        product(0, slice(0, P), halves[1], y_first[1][:], "turned11")
+        for a in range(2):
+            nc.vector.tensor_tensor(
+                windows[0][:].indirect(list_half(dst_sb, a)), y_first[a][:], gate_sb[:, halves[a]], MULT
+            )
+        for i in range(2):
+            weave(nc.scalar.copy, w_woven[2][:, i * P : (i + 1) * P, :], w_late[:, :, i * P : (i + 1) * P])
+        quantize(nc, w_codes[2][:], w_scales[2][:], w_woven[2][:])
+
+        ys = [None, sb.tile([P, S], F32, name="y1", tag="late")]
+        ys.extend(sb.tile([P, S], F32, name="y%d" % g, align_bytes=64) for g in (2, 3))
+        product(1, slice(0, P), slice(0, S), ys[1][:], "back00")
+        product(2, slice(0, P), slice(0, S), ys[2][:], "turned00")
+        product(2, slice(P, 2 * P), slice(0, S), ys[3][:], "turned01")
+        for g in range(1, GROUPS):
+            nc.vector.tensor_tensor(windows[g][:].indirect(dst_sb[:]), ys[g][:], gate_sb[:], MULT)
+
+        codes_early = sb.tile([P, GROUPS - 1, QUARTER], U32, name="codes_early", tag="y3", align_bytes=64)
+        codes_last = sb.tile([P, QUARTER], U32, name="codes_last", align_bytes=64)
+        out_scales = sb.tile([P, GROUPS, QUARTER], U8, name="out_scales", align_bytes=64)
+
+        for g in range(GROUPS):
+            last = g == GROUPS - 1
+            nc.sync.dma_start(out_0[g * P : (g + 1) * P, :], windows[g][:])
+            regrouped = sb.tile([P, QUARTER, PACK], BF16, name="regrouped%d" % g, align_bytes=64)
+            pairs = []
+            for h in range(2):
+                copy = nc.vector.tensor_copy if last and h == 1 else nc.scalar.copy
+                turned = ps.tile([P, 4, P], F32, name="turned", tag="turned%d%d" % (g % 2, h))
+                for q in range(4):
+                    c0 = q * QUARTER + h * P
+                    nc.tensor.transpose(turned[:, q, :], windows[g][:, c0 : c0 + P], ident[:])
+                pair = ring.tile([P, 2, P, 2], BF16, name="pair")
+                copy(pair[:], turned[:].rearrange("c q (l u e) -> c u (q l) e", u=2, e=2))
+                pairs.append(pair)
+            for h in range(2):
+                copy = nc.vector.tensor_copy if last and h == 1 else nc.scalar.copy
+                pair_words = pairs[h][:].rearrange("c u m e -> c (u m e)").bitcast(F32)
+                back = ps.tile([P, 2, P], F32, name="back", tag="back%d%d" % (g % 2, h))
+                for u in range(2):
+                    nc.tensor.transpose(back[:, u, :], pair_words[:, u * P : (u + 1) * P], ident[:])
+                cols = slice(h * P, (h + 1) * P)
+                target = regrouped[:, cols, :].rearrange("m c t -> m (c t)").bitcast(F32)
+                copy(target.rearrange("m (c u) -> m c u", u=2), back[:].rearrange("m u c -> m c u"))
+                if last:
+                    quantize(nc, codes_last[:, cols], out_scales[:, g, cols], regrouped[:, cols, :])
+            if not last:
+                quantize(nc, codes_early[:, g, :], out_scales[:, g, :], regrouped[:])
+            if g == GROUPS - 2:
+                for q in range(4):
+                    nc.sync.dma_start(words_hbm[q, :, 0 : GROUPS - 1, :], codes_early[32 * q : 32 * q + 32].bitcast(I32))
+
+        for q in range(4):
+            queue = nc.sync if q % 2 == 0 else nc.scalar
+            queue.dma_start(words_hbm[q, :, GROUPS - 1, :], codes_last[32 * q : 32 * q + 32, :].bitcast(I32))
+        for q in range(4):
+            queue = nc.sync if q % 2 == 0 else nc.scalar
+            queue.dma_start(scales_hbm[q], out_scales[32 * q : 32 * q + 4].bitcast(I32))

@@ -51,7 +51,7 @@ def tile_picked_route2_linnone_lo_kernel(
         offs_sb = sb.tile([P, LIST_COLS], U16, name="offs_sb")
         dst_sb = sb.tile([P, LIST_COLS], U16, name="dst_sb")
         x_sb = [sb.tile([P, T], F32, name="x%d" % j) for j in range(PACK)]
-        w_first = [sb.tile([P, PACK, P], F32, name="w%d" % g) for g in range(2)]
+        w_first = [sb.tile([P, PACK, P], F32, name="w%d" % g, align_bytes=64) for g in range(2)]
         w_late = sb.tile([P, PACK, 2 * P], F32, name="w_late", tag="late")
         gate_sb = sb.tile([P, S], F32, name="gate_sb")
 
@@ -65,77 +65,87 @@ def tile_picked_route2_linnone_lo_kernel(
         nc.sync.dma_start(dst_sb[:], dst)
         nc.sync.dma_start(w_late[:], w_rows[:, :, 2 * P :])
 
-        windows = [sb.tile([P, U], F32, name="window%d" % g) for g in range(GROUPS)]
-        nc.vector.memset(windows[0][:], 0.0)
+        windows = [sb.tile([P, U], F32, name="window%d" % g) for g in range(GROUPS - 1)]
+        for g in range(GROUPS - 1):
+            nc.vector.memset(windows[g][:].bitcast(I32), 0)
         ident = sb.tile([P, P], F32, name="ident")
         make_identity(nc, ident[:])
-        for g in range(1, GROUPS):
-            nc.gpsimd.memset(windows[g][:], 0.0)
 
-        def list_half(list_sb, a):
-            return list_sb[:, a * LIST_COLS // 2 : (a + 1) * LIST_COLS // 2]
-
-        picked01 = [sb.tile([P, 2, HALF], F32, name="picked01_%d" % a) for a in range(2)]
-        x_woven = [sb.tile([P, HALF, PACK], BF16, name="x_woven%d" % a, align_bytes=64) for a in range(2)]
-        for j in range(2):
-            for a in range(2):
-                nc.vector.tensor_copy(picked01[a][:, j, :], x_sb[j][:].indirect(list_half(offs_sb, a)))
-        for a in range(2):
-            weave(nc.scalar.copy, x_woven[a][:, :, 0:2], picked01[a][:])
-
-        def gather_woven(j, a):
-            nc.vector.tensor_copy(x_woven[a][:, :, j], x_sb[j][:].indirect(list_half(offs_sb, a)))
-
-        x_codes = sb.tile([P, S], U32, name="x_codes", align_bytes=64)
-        x_scales = sb.tile([P, S], U8, name="x_scales", align_bytes=64)
+        halves = [slice(0, HALF), slice(HALF, S)]
+        list_halves = [slice(0, LIST_COLS // 2), slice(LIST_COLS // 2, LIST_COLS)]
+        first_pair = sb.tile([P, 2, HALF], F32, name="first_pair")
+        second = sb.tile([P, PACK, HALF], F32, name="second")
+        x_woven = [sb.tile([P, HALF, PACK], BF16, name="x_woven0", align_bytes=64)]
+        x_codes = [sb.tile([P, HALF], U32, name="x_codes%d" % a, align_bytes=64) for a in range(2)]
+        x_scales = [sb.tile([P, HALF], U8, name="x_scales%d" % a, align_bytes=64) for a in range(2)]
         widths = [P, P, 2 * P]
         w_woven = [sb.tile([P, n, PACK], BF16, name="w_woven%d" % i, align_bytes=64) for i, n in enumerate(widths)]
         w_codes = [sb.tile([P, n], U32, name="w_codes%d" % i, align_bytes=64) for i, n in enumerate(widths)]
         w_scales = [sb.tile([P, n], U8, name="w_scales%d" % i, align_bytes=64) for i, n in enumerate(widths)]
 
-        def product(piece, w_cols, entries, y, bank):
-            acc = ps.tile([P, S], F32, name="acc", tag=bank)
-            n = entries.stop - entries.start
+        def gather(out, j, list_cols):
+            nc.vector.tensor_copy(out, x_sb[j][:].indirect(offs_sb[:, list_cols]))
+
+        def product(piece, w_cols, a, y, bank, copy):
+            acc = ps.tile([P, HALF], F32, name="acc", tag=bank)
             nc.tensor.matmul_mx(
-                out=acc[:, 0:n],
+                out=acc[:],
                 lhsT=w_codes[piece][:, w_cols].bitcast(FP8X4),
                 lhsT_scale=w_scales[piece][:, w_cols],
-                rhs=x_codes[:, entries].bitcast(FP8X4),
-                rhs_scale=x_scales[:, entries],
+                rhs=x_codes[a][:].bitcast(FP8X4),
+                rhs_scale=x_scales[a][:],
                 start=True,
                 stop=True,
             )
-            nc.scalar.copy(y, acc[:, 0:n])
+            copy(y, acc[:])
 
-        halves = [slice(0, HALF), slice(HALF, S)]
-        gather_woven(2, 0)
-        gather_woven(2, 1)
+        def scatter(g, y, entries, list_cols):
+            nc.vector.tensor_tensor(windows[g][:].indirect(dst_sb[:, list_cols]), y, gate_sb[:, entries], MULT)
+
+        for j in range(2):
+            gather(first_pair[:, j, :], j, list_halves[0])
+            gather(second[:, j, :], j, list_halves[1])
+        weave(nc.scalar.copy, x_woven[0][:, :, 0:2], first_pair[:])
+        gather(x_woven[0][:, :, 2], 2, list_halves[0])
+        gather(second[:, 2, :], 2, list_halves[1])
         weave(nc.scalar.copy, w_woven[0][:], w_first[0][:])
-        gather_woven(3, 0)
         quantize(nc, w_codes[0][:], w_scales[0][:], w_woven[0][:])
-        quantize(nc, x_codes[:, halves[0]], x_scales[:, halves[0]], x_woven[0][:])
-        gather_woven(3, 1)
-        quantize(nc, x_codes[:, halves[1]], x_scales[:, halves[1]], x_woven[1][:])
-        y_first = [sb.tile([P, HALF], F32, name="y_first%d" % a) for a in range(2)]
-        product(0, slice(0, P), halves[0], y_first[0][:], "turned10")
+        gather(x_woven[0][:, :, 3], 3, list_halves[0])
+        quantize(nc, x_codes[0][:], x_scales[0][:], x_woven[0][:])
+        for i in range(2):
+            cols = slice(LIST_COLS // 2 + i * LIST_COLS // 4, LIST_COLS // 2 + (i + 1) * LIST_COLS // 4)
+            gather(second[:, 3, i * HALF // 2 : (i + 1) * HALF // 2], 3, cols)
+
         weave(nc.scalar.copy, w_woven[1][:], w_first[1][:])
         quantize(nc, w_codes[1][:], w_scales[1][:], w_woven[1][:])
-        product(0, slice(0, P), halves[1], y_first[1][:], "turned11")
-        for a in range(2):
-            nc.vector.tensor_tensor(
-                windows[0][:].indirect(list_half(dst_sb, a)), y_first[a][:], gate_sb[:, halves[a]], MULT
-            )
+        y_half = [
+            [
+                sb.tile([P, HALF], F32, name="y0_first", tag="w_woven1", align_bytes=64),
+                sb.tile([P, HALF], F32, name="y1_first"),
+            ]
+        ]
+        product(0, slice(0, P), 0, y_half[0][0][:], "back00", nc.vector.tensor_copy)
+        scatter(0, y_half[0][0][:], halves[0], list_halves[0])
+        x_woven.append(sb.tile([P, HALF, PACK], BF16, name="x_woven1", tag="w1", align_bytes=64))
+        weave(nc.scalar.copy, x_woven[1][:], second[:])
+        quantize(nc, x_codes[1][:], x_scales[1][:], x_woven[1][:])
+        windows.append(sb.tile([P, U], F32, name="window_last", tag="w1", align_bytes=64))
+        nc.gpsimd.memset(windows[GROUPS - 1][:], 0.0)
+        product(1, slice(0, P), 0, y_half[0][1][:], "back01", nc.scalar.copy)
+        scatter(1, y_half[0][1][:], halves[0], list_halves[0])
         for i in range(2):
             weave(nc.scalar.copy, w_woven[2][:, i * P : (i + 1) * P, :], w_late[:, :, i * P : (i + 1) * P])
         quantize(nc, w_codes[2][:], w_scales[2][:], w_woven[2][:])
 
-        ys = [None, sb.tile([P, S], F32, name="y1", tag="late")]
-        ys.extend(sb.tile([P, S], F32, name="y%d" % g, align_bytes=64) for g in (2, 3))
-        product(1, slice(0, P), slice(0, S), ys[1][:], "back00")
-        product(2, slice(0, P), slice(0, S), ys[2][:], "turned00")
-        product(2, slice(P, 2 * P), slice(0, S), ys[3][:], "turned01")
-        for g in range(1, GROUPS):
-            nc.vector.tensor_tensor(windows[g][:].indirect(dst_sb[:]), ys[g][:], gate_sb[:], MULT)
+        y_half.append([sb.tile([P, HALF], F32, name="y0_second", tag="late"), sb.tile([P, HALF], F32, name="y1_second")])
+        for g in range(2):
+            product(g, slice(0, P), 1, y_half[1][g][:], "back1%d" % g, nc.scalar.copy)
+            scatter(g, y_half[1][g][:], halves[1], list_halves[1])
+        for g in range(2, GROUPS):
+            y = sb.tile([P, S], F32, name="y%d" % g, align_bytes=64)
+            for a in range(2):
+                product(2, slice((g - 2) * P, (g - 1) * P), a, y[:, halves[a]], "turned%d%d" % (g - 2, a), nc.scalar.copy)
+            scatter(g, y[:], slice(0, S), slice(0, LIST_COLS))
 
         codes_early = sb.tile([P, GROUPS - 1, QUARTER], U32, name="codes_early", tag="y3", align_bytes=64)
         codes_last = sb.tile([P, QUARTER], U32, name="codes_last", align_bytes=64)
@@ -147,23 +157,29 @@ def tile_picked_route2_linnone_lo_kernel(
             regrouped = sb.tile([P, QUARTER, PACK], BF16, name="regrouped%d" % g, align_bytes=64)
             pairs = []
             for h in range(2):
-                copy = nc.vector.tensor_copy if last and h == 1 else nc.scalar.copy
-                turned = ps.tile([P, 4, P], F32, name="turned", tag="turned%d%d" % (g % 2, h))
-                for q in range(4):
-                    c0 = q * QUARTER + h * P
-                    nc.tensor.transpose(turned[:, q, :], windows[g][:, c0 : c0 + P], ident[:])
                 pair = ring.tile([P, 2, P, 2], BF16, name="pair")
-                copy(pair[:], turned[:].rearrange("c q (l u e) -> c u (q l) e", u=2, e=2))
+                if last:
+                    parts = [(range(0, 2), 0, nc.vector.tensor_copy), (range(2, 4), 1, nc.scalar.copy)]
+                else:
+                    parts = [(range(4), g % 2, nc.scalar.copy)]
+                for blocks, bank, copy in parts:
+                    turned = ps.tile([P, len(blocks), P], F32, name="turned", tag="turned%d%d" % (bank, h))
+                    for i, q in enumerate(blocks):
+                        c0 = q * QUARTER + h * P
+                        nc.tensor.transpose(turned[:, i, :], windows[g][:, c0 : c0 + P], ident[:])
+                    copy(
+                        pair[:, :, 32 * blocks.start : 32 * blocks.stop, :],
+                        turned[:].rearrange("c q (l u e) -> c u (q l) e", u=2, e=2),
+                    )
                 pairs.append(pair)
             for h in range(2):
-                copy = nc.vector.tensor_copy if last and h == 1 else nc.scalar.copy
                 pair_words = pairs[h][:].rearrange("c u m e -> c (u m e)").bitcast(F32)
                 back = ps.tile([P, 2, P], F32, name="back", tag="back%d%d" % (g % 2, h))
                 for u in range(2):
                     nc.tensor.transpose(back[:, u, :], pair_words[:, u * P : (u + 1) * P], ident[:])
                 cols = slice(h * P, (h + 1) * P)
                 target = regrouped[:, cols, :].rearrange("m c t -> m (c t)").bitcast(F32)
-                copy(target.rearrange("m (c u) -> m c u", u=2), back[:].rearrange("m u c -> m c u"))
+                nc.scalar.copy(target.rearrange("m (c u) -> m c u", u=2), back[:].rearrange("m u c -> m c u"))
                 if last:
                     quantize(nc, codes_last[:, cols], out_scales[:, g, cols], regrouped[:, cols, :])
             if not last:

@@ -55,8 +55,9 @@ def tile_picked_route2_linnone_lo_kernel(
         w_late = sb.tile([P, PACK, 2 * P], F32, name="w_late", tag="late")
         gate_sb = sb.tile([P, S], F32, name="gate_sb")
 
+        nc.sync.dma_start(x_sb[0][:], x_rows[:, 0, :])
         nc.sync.dma_start(offs_sb[:], offs)
-        for j in range(PACK - 1):
+        for j in range(1, PACK - 1):
             nc.sync.dma_start(x_sb[j][:], x_rows[:, j, :])
         nc.sync.dma_start(w_first[0][:], w_rows[:, :, 0:P])
         nc.sync.dma_start(x_sb[PACK - 1][:], x_rows[:, PACK - 1, :])
@@ -71,85 +72,98 @@ def tile_picked_route2_linnone_lo_kernel(
         ident = sb.tile([P, P], F32, name="ident")
         make_identity(nc, ident[:])
 
-        halves = [slice(0, HALF), slice(HALF, S)]
-        list_halves = [slice(0, LIST_COLS // 2), slice(LIST_COLS // 2, LIST_COLS)]
-        first_pair = sb.tile([P, 2, HALF], F32, name="first_pair")
-        second = sb.tile([P, PACK, HALF], F32, name="second")
-        x_woven = [sb.tile([P, HALF, PACK], BF16, name="x_woven0", align_bytes=64)]
-        x_codes = [sb.tile([P, HALF], U32, name="x_codes%d" % a, align_bytes=64) for a in range(2)]
-        x_scales = [sb.tile([P, HALF], U8, name="x_scales%d" % a, align_bytes=64) for a in range(2)]
-        widths = [P, P, 2 * P]
-        w_woven = [sb.tile([P, n, PACK], BF16, name="w_woven%d" % i, align_bytes=64) for i, n in enumerate(widths)]
-        w_codes = [sb.tile([P, n], U32, name="w_codes%d" % i, align_bytes=64) for i, n in enumerate(widths)]
-        w_scales = [sb.tile([P, n], U8, name="w_scales%d" % i, align_bytes=64) for i, n in enumerate(widths)]
+        pieces = [slice(0, P), slice(P, 2 * P), slice(2 * P, S)]
+        rest = slice(P, S)
+        first_pair = sb.tile([P, 2, P], F32, name="first_pair")
+        rest_raw = sb.tile([P, PACK, S - P], F32, name="rest_raw", align_bytes=64)
+        first_woven = rest_raw[:, PACK - 1, P:].bitcast(BF16).rearrange("p (c t) -> p c t", t=PACK)
+        x_widths = [piece.stop - piece.start for piece in pieces]
+        x_codes = [sb.tile([P, n], U32, name="x_codes%d" % a, align_bytes=64) for a, n in enumerate(x_widths)]
+        x_scales = [sb.tile([P, n], U8, name="x_scales%d" % a, align_bytes=64) for a, n in enumerate(x_widths)]
+        w_widths = [P, P, 2 * P]
+        w_woven = [sb.tile([P, n, PACK], BF16, name="w_woven%d" % i, align_bytes=64) for i, n in enumerate(w_widths)]
+        w_codes = [sb.tile([P, n], U32, name="w_codes%d" % i, align_bytes=64) for i, n in enumerate(w_widths)]
+        w_scales = [sb.tile([P, n], U8, name="w_scales%d" % i, align_bytes=64) for i, n in enumerate(w_widths)]
 
-        def gather(out, j, list_cols):
-            nc.vector.tensor_copy(out, x_sb[j][:].indirect(offs_sb[:, list_cols]))
+        def list_cols(entries):
+            return slice(entries.start // 16, entries.stop // 16)
 
-        def product(piece, w_cols, a, y, bank, copy):
-            acc = ps.tile([P, HALF], F32, name="acc", tag=bank)
-            nc.tensor.matmul_mx(
-                out=acc[:],
-                lhsT=w_codes[piece][:, w_cols].bitcast(FP8X4),
-                lhsT_scale=w_scales[piece][:, w_cols],
-                rhs=x_codes[a][:].bitcast(FP8X4),
-                rhs_scale=x_scales[a][:],
-                start=True,
-                stop=True,
-            )
+        def in_rest(entries):
+            return slice(entries.start - rest.start, entries.stop - rest.start)
+
+        def gather(out, j, entries):
+            nc.vector.tensor_copy(out, x_sb[j][:].indirect(offs_sb[:, list_cols(entries)]))
+
+        def product(g, parts, y, bank, copy):
+            held, first_col = (g, 0) if g < 2 else (2, (g - 2) * P)
+            w_cols = slice(first_col, first_col + P)
+            acc = ps.tile([P, sum(x_widths[a] for a in parts)], F32, name="acc", tag=bank)
+            for a in parts:
+                start = pieces[a].start - pieces[parts[0]].start
+                nc.tensor.matmul_mx(
+                    out=acc[:, start : start + x_widths[a]],
+                    lhsT=w_codes[held][:, w_cols].bitcast(FP8X4),
+                    lhsT_scale=w_scales[held][:, w_cols],
+                    rhs=x_codes[a][:].bitcast(FP8X4),
+                    rhs_scale=x_scales[a][:],
+                    start=True,
+                    stop=True,
+                )
             copy(y, acc[:])
 
-        def scatter(g, y, entries, list_cols):
-            nc.vector.tensor_tensor(windows[g][:].indirect(dst_sb[:, list_cols]), y, gate_sb[:, entries], MULT)
+        def scatter(g, y, entries):
+            nc.vector.tensor_tensor(windows[g][:].indirect(dst_sb[:, list_cols(entries)]), y, gate_sb[:, entries], MULT)
 
         for j in range(2):
-            gather(first_pair[:, j, :], j, list_halves[0])
-            gather(second[:, j, :], j, list_halves[1])
-        weave(nc.scalar.copy, x_woven[0][:, :, 0:2], first_pair[:])
-        gather(x_woven[0][:, :, 2], 2, list_halves[0])
-        gather(second[:, 2, :], 2, list_halves[1])
+            gather(first_pair[:, j, :], j, pieces[0])
+            gather(rest_raw[:, j, :], j, rest)
+        weave(nc.scalar.copy, first_woven[:, :, 0:2], first_pair[:])
+        gather(first_woven[:, :, 2], 2, pieces[0])
+        gather(rest_raw[:, 2, :], 2, rest)
         weave(nc.scalar.copy, w_woven[0][:], w_first[0][:])
         quantize(nc, w_codes[0][:], w_scales[0][:], w_woven[0][:])
-        gather(x_woven[0][:, :, 3], 3, list_halves[0])
-        quantize(nc, x_codes[0][:], x_scales[0][:], x_woven[0][:])
-        for i in range(2):
-            cols = slice(LIST_COLS // 2 + i * LIST_COLS // 4, LIST_COLS // 2 + (i + 1) * LIST_COLS // 4)
-            gather(second[:, 3, i * HALF // 2 : (i + 1) * HALF // 2], 3, cols)
-
+        gather(first_woven[:, :, 3], 3, pieces[0])
+        quantize(nc, x_codes[0][:], x_scales[0][:], first_woven)
+        for a in (1, 2):
+            gather(rest_raw[:, 3, in_rest(pieces[a])], 3, pieces[a])
         weave(nc.scalar.copy, w_woven[1][:], w_first[1][:])
         quantize(nc, w_codes[1][:], w_scales[1][:], w_woven[1][:])
-        y_half = [
-            [
-                sb.tile([P, HALF], F32, name="y0_first", tag="w_woven1", align_bytes=64),
-                sb.tile([P, HALF], F32, name="y1_first"),
-            ]
-        ]
-        product(0, slice(0, P), 0, y_half[0][0][:], "back00", nc.vector.tensor_copy)
-        scatter(0, y_half[0][0][:], halves[0], list_halves[0])
-        x_woven.append(sb.tile([P, HALF, PACK], BF16, name="x_woven1", tag="w1", align_bytes=64))
-        weave(nc.scalar.copy, x_woven[1][:], second[:])
-        quantize(nc, x_codes[1][:], x_scales[1][:], x_woven[1][:])
-        windows.append(sb.tile([P, U], F32, name="window_last", tag="w1", align_bytes=64))
-        nc.gpsimd.memset(windows[GROUPS - 1][:], 0.0)
-        product(1, slice(0, P), 0, y_half[0][1][:], "back01", nc.scalar.copy)
-        scatter(1, y_half[0][1][:], halves[0], list_halves[0])
+
+        rest_woven = sb.tile([P, S - P, PACK], BF16, name="rest_woven", tag="w1", align_bytes=64)
+        weave(nc.scalar.copy, rest_woven[:, in_rest(pieces[1]), :], rest_raw[:, :, in_rest(pieces[1])])
+
+        y00 = sb.tile([P, P], F32, name="y00")
+        product(0, [0], y00[:], "back00", nc.scalar.copy)
+        scatter(0, y00[:], pieces[0])
+        y10 = sb.tile([P, P], F32, name="y10")
+        product(1, [0], y10[:], "back01", nc.scalar.copy)
+        weave(nc.scalar.copy, rest_woven[:, in_rest(pieces[2]), :], rest_raw[:, :, in_rest(pieces[2])])
+        quantize(nc, x_codes[1][:], x_scales[1][:], rest_woven[:, in_rest(pieces[1]), :])
+        scatter(1, y10[:], pieces[0])
+        quantize(nc, x_codes[2][:], x_scales[2][:], rest_woven[:, in_rest(pieces[2]), :])
+        for g in range(2):
+            y = sb.tile([P, P], F32, name="y%d1" % g)
+            product(g, [1], y[:], "back1%d" % g, nc.scalar.copy)
+            scatter(g, y[:], pieces[1])
+
         for i in range(2):
             weave(nc.scalar.copy, w_woven[2][:, i * P : (i + 1) * P, :], w_late[:, :, i * P : (i + 1) * P])
         quantize(nc, w_codes[2][:], w_scales[2][:], w_woven[2][:])
-
-        y_half.append([sb.tile([P, HALF], F32, name="y0_second", tag="late"), sb.tile([P, HALF], F32, name="y1_second")])
+        windows.append(sb.tile([P, U], F32, name="window_last", tag="w_woven2", align_bytes=64))
+        nc.gpsimd.memset(windows[GROUPS - 1][:], 0.0)
         for g in range(2):
-            product(g, slice(0, P), 1, y_half[1][g][:], "back1%d" % g, nc.scalar.copy)
-            scatter(g, y_half[1][g][:], halves[1], list_halves[1])
+            y = sb.tile([P, 2 * P], F32, name="y%d2" % g, tag="late" if g == 0 else "y12")
+            product(g, [2], y[:], "turned1%d" % g, nc.scalar.copy)
+            scatter(g, y[:], pieces[2])
         for g in range(2, GROUPS):
             y = sb.tile([P, S], F32, name="y%d" % g, align_bytes=64)
-            for a in range(2):
-                product(2, slice((g - 2) * P, (g - 1) * P), a, y[:, halves[a]], "turned%d%d" % (g - 2, a), nc.scalar.copy)
-            scatter(g, y[:], slice(0, S), slice(0, LIST_COLS))
+            product(g, [0, 1, 2], y[:], "turned0%d" % (g - 2), nc.scalar.copy)
+            scatter(g, y[:], slice(0, S))
 
         codes_early = sb.tile([P, GROUPS - 1, QUARTER], U32, name="codes_early", tag="y3", align_bytes=64)
+        scales_early = sb.tile([P, GROUPS - 1, QUARTER], U8, name="scales_early", align_bytes=64)
         codes_last = sb.tile([P, QUARTER], U32, name="codes_last", align_bytes=64)
-        out_scales = sb.tile([P, GROUPS, QUARTER], U8, name="out_scales", align_bytes=64)
+        scales_last = sb.tile([P, QUARTER], U8, name="scales_last", align_bytes=64)
 
         for g in range(GROUPS):
             last = g == GROUPS - 1
@@ -158,12 +172,12 @@ def tile_picked_route2_linnone_lo_kernel(
             pairs = []
             for h in range(2):
                 pair = ring.tile([P, 2, P, 2], BF16, name="pair")
-                if last:
-                    parts = [(range(0, 2), 0, nc.vector.tensor_copy), (range(2, 4), 1, nc.scalar.copy)]
+                if last and h == 1:
+                    parts = [(range(0, 2), "back00", nc.vector.tensor_copy), (range(2, 4), "back01", nc.scalar.copy)]
                 else:
-                    parts = [(range(4), g % 2, nc.scalar.copy)]
+                    parts = [(range(4), "turned01" if last else "turned%d%d" % (g % 2, h), nc.scalar.copy)]
                 for blocks, bank, copy in parts:
-                    turned = ps.tile([P, len(blocks), P], F32, name="turned", tag="turned%d%d" % (bank, h))
+                    turned = ps.tile([P, len(blocks), P], F32, name="turned", tag=bank)
                     for i, q in enumerate(blocks):
                         c0 = q * QUARTER + h * P
                         nc.tensor.transpose(turned[:, i, :], windows[g][:, c0 : c0 + P], ident[:])
@@ -181,16 +195,18 @@ def tile_picked_route2_linnone_lo_kernel(
                 target = regrouped[:, cols, :].rearrange("m c t -> m (c t)").bitcast(F32)
                 nc.scalar.copy(target.rearrange("m (c u) -> m c u", u=2), back[:].rearrange("m u c -> m c u"))
                 if last:
-                    quantize(nc, codes_last[:, cols], out_scales[:, g, cols], regrouped[:, cols, :])
+                    quantize(nc, codes_last[:, cols], scales_last[:, cols], regrouped[:, cols, :])
             if not last:
-                quantize(nc, codes_early[:, g, :], out_scales[:, g, :], regrouped[:])
+                quantize(nc, codes_early[:, g, :], scales_early[:, g, :], regrouped[:])
             if g == GROUPS - 2:
                 for q in range(4):
-                    nc.sync.dma_start(words_hbm[q, :, 0 : GROUPS - 1, :], codes_early[32 * q : 32 * q + 32].bitcast(I32))
+                    nc.sync.dma_start(scales_hbm[q, :, 0 : g + 1, :], scales_early[32 * q : 32 * q + 4].bitcast(I32))
+                for q in range(4):
+                    nc.sync.dma_start(words_hbm[q, :, 0 : g + 1, :], codes_early[32 * q : 32 * q + 32].bitcast(I32))
 
         for q in range(4):
             queue = nc.sync if q % 2 == 0 else nc.scalar
             queue.dma_start(words_hbm[q, :, GROUPS - 1, :], codes_last[32 * q : 32 * q + 32, :].bitcast(I32))
         for q in range(4):
             queue = nc.sync if q % 2 == 0 else nc.scalar
-            queue.dma_start(scales_hbm[q], out_scales[32 * q : 32 * q + 4].bitcast(I32))
+            queue.dma_start(scales_hbm[q, :, GROUPS - 1, :], scales_last[32 * q : 32 * q + 4, :].bitcast(I32))

from contextlib import ExitStack

import concourse.mybir as mybir
from concourse.masks import make_identity

K, T, S, N, U = 512, 1024, 512, 512, 1024
FLOPS = 2 * K * N * S

F32 = mybir.dt.float32
BF16 = mybir.dt.bfloat16
I32 = mybir.dt.int32
U32 = mybir.dt.uint32
U16 = mybir.dt.uint16
U8 = mybir.dt.uint8
FP8X4 = mybir.dt.float8_e4m3fn_x4
MULT = mybir.AluOpType.mult

P = 128
PACK = 4
HALF = S // 2
LIST_COLS = S // 16
GROUPS = N // P
QUARTER = U // 4


def weave(engine_copy, out, in_):
    engine_copy(
        out.rearrange("p (c i) t -> p c t i", i=4),
        in_.rearrange("p t (c i) -> p c t i", i=4),
    )


def quantize(nc, codes, scales, woven):
    nc.vector.quantize_mx(out=codes.bitcast(FP8X4), scales=scales, in_=woven.rearrange("p c t -> p (c t)"))


def tile_picked_route2_linnone_lo_kernel(
    tc, xT, gate, w1, offs, dst, out_0, out_1, out_2
):
    nc = tc.nc
    x_rows = xT.rearrange("(p j) t -> p j t", j=PACK)
    w_rows = w1.rearrange("(p j) n -> p j n", j=PACK)
    words_hbm = out_1[0].rearrange("l c r -> l (c r)").bitcast(I32).rearrange("(g l) (q c) -> q l g c", g=GROUPS, q=4)
    scales_hbm = out_2[0].bitcast(I32).rearrange("(g b) (q c) -> q b g c", g=GROUPS, q=4)

    with ExitStack() as ctx:
        sb = ctx.enter_context(tc.tile_pool(name="sb", bufs=1))
        ring = ctx.enter_context(tc.tile_pool(name="ring", bufs=4))
        ps = ctx.enter_context(tc.psum_pool(name="ps", bufs=1))

        offs_sb = sb.tile([P, LIST_COLS], U16, name="offs_sb")
        dst_sb = sb.tile([P, LIST_COLS], U16, name="dst_sb")
        x_sb = [sb.tile([P, T], F32, name="x%d" % j) for j in range(PACK)]
        w_first = [sb.tile([P, PACK, P], F32, name="w%d" % g, align_bytes=64) for g in range(2)]
        w_late = sb.tile([P, PACK, 2 * P], F32, name="w_late", tag="late")
        gate_sb = sb.tile([P, S], F32, name="gate_sb")

        nc.sync.dma_start(x_sb[0][:], x_rows[:, 0, :])
        nc.sync.dma_start(offs_sb[:], offs)
        for j in range(1, PACK - 1):
            nc.sync.dma_start(x_sb[j][:], x_rows[:, j, :])
        nc.sync.dma_start(w_first[0][:], w_rows[:, :, 0:P])
        nc.sync.dma_start(x_sb[PACK - 1][:], x_rows[:, PACK - 1, :])
        nc.sync.dma_start(w_first[1][:], w_rows[:, :, P : 2 * P])
        nc.sync.dma_start(gate_sb[:], gate)
        nc.sync.dma_start(dst_sb[:], dst)
        nc.sync.dma_start(w_late[:], w_rows[:, :, 2 * P :])

        windows = [sb.tile([P, U], F32, name="window%d" % g) for g in range(GROUPS - 1)]
        for g in range(GROUPS - 1):
            nc.vector.memset(windows[g][:].bitcast(I32), 0)
        ident = sb.tile([P, P], F32, name="ident")
        make_identity(nc, ident[:])

        pieces = [slice(0, P), slice(P, 2 * P), slice(2 * P, S)]
        rest = slice(P, S)
        first_pair = sb.tile([P, 2, P], F32, name="first_pair")
        rest_raw = sb.tile([P, PACK, S - P], F32, name="rest_raw", align_bytes=64)
        first_woven = rest_raw[:, PACK - 1, P:].bitcast(BF16).rearrange("p (c t) -> p c t", t=PACK)
        x_widths = [piece.stop - piece.start for piece in pieces]
        x_codes = [sb.tile([P, n], U32, name="x_codes%d" % a, align_bytes=64) for a, n in enumerate(x_widths)]
        x_scales = [sb.tile([P, n], U8, name="x_scales%d" % a, align_bytes=64) for a, n in enumerate(x_widths)]
        w_widths = [P, P, 2 * P]
        w_woven = [sb.tile([P, n, PACK], BF16, name="w_woven%d" % i, align_bytes=64) for i, n in enumerate(w_widths)]
        w_codes = [sb.tile([P, n], U32, name="w_codes%d" % i, align_bytes=64) for i, n in enumerate(w_widths)]
        w_scales = [sb.tile([P, n], U8, name="w_scales%d" % i, align_bytes=64) for i, n in enumerate(w_widths)]

        def list_cols(entries):
            return slice(entries.start // 16, entries.stop // 16)

        def in_rest(entries):
            return slice(entries.start - rest.start, entries.stop - rest.start)

        def gather(out, j, entries):
            nc.vector.tensor_copy(out, x_sb[j][:].indirect(offs_sb[:, list_cols(entries)]))

        def product(g, parts, y, bank, copy):
            held, first_col = (g, 0) if g < 2 else (2, (g - 2) * P)
            w_cols = slice(first_col, first_col + P)
            acc = ps.tile([P, sum(x_widths[a] for a in parts)], F32, name="acc", tag=bank)
            for a in parts:
                start = pieces[a].start - pieces[parts[0]].start
                nc.tensor.matmul_mx(
                    out=acc[:, start : start + x_widths[a]],
                    lhsT=w_codes[held][:, w_cols].bitcast(FP8X4),
                    lhsT_scale=w_scales[held][:, w_cols],
                    rhs=x_codes[a][:].bitcast(FP8X4),
                    rhs_scale=x_scales[a][:],
                    start=True,
                    stop=True,
                )
            copy(y, acc[:])

        def scatter(g, y, entries):
            nc.vector.tensor_tensor(windows[g][:].indirect(dst_sb[:, list_cols(entries)]), y, gate_sb[:, entries], MULT)

        for j in range(2):
            gather(first_pair[:, j, :], j, pieces[0])
            gather(rest_raw[:, j, :], j, rest)
        weave(nc.scalar.copy, first_woven[:, :, 0:2], first_pair[:])
        gather(first_woven[:, :, 2], 2, pieces[0])
        gather(rest_raw[:, 2, :], 2, rest)
        weave(nc.scalar.copy, w_woven[0][:], w_first[0][:])
        quantize(nc, w_codes[0][:], w_scales[0][:], w_woven[0][:])
        gather(first_woven[:, :, 3], 3, pieces[0])
        quantize(nc, x_codes[0][:], x_scales[0][:], first_woven)
        for a in (1, 2):
            gather(rest_raw[:, 3, in_rest(pieces[a])], 3, pieces[a])
        weave(nc.scalar.copy, w_woven[1][:], w_first[1][:])
        quantize(nc, w_codes[1][:], w_scales[1][:], w_woven[1][:])

        rest_woven = sb.tile([P, S - P, PACK], BF16, name="rest_woven", tag="w1", align_bytes=64)
        weave(nc.scalar.copy, rest_woven[:, in_rest(pieces[1]), :], rest_raw[:, :, in_rest(pieces[1])])

        y00 = sb.tile([P, P], F32, name="y00")
        product(0, [0], y00[:], "back00", nc.scalar.copy)
        scatter(0, y00[:], pieces[0])
        y10 = sb.tile([P, P], F32, name="y10")
        product(1, [0], y10[:], "back01", nc.scalar.copy)
        weave(nc.scalar.copy, rest_woven[:, in_rest(pieces[2]), :], rest_raw[:, :, in_rest(pieces[2])])
        quantize(nc, x_codes[1][:], x_scales[1][:], rest_woven[:, in_rest(pieces[1]), :])
        scatter(1, y10[:], pieces[0])
        quantize(nc, x_codes[2][:], x_scales[2][:], rest_woven[:, in_rest(pieces[2]), :])
        for g in range(2):
            y = sb.tile([P, P], F32, name="y%d1" % g)
            product(g, [1], y[:], "back1%d" % g, nc.scalar.copy)
            scatter(g, y[:], pieces[1])

        for i in range(2):
            weave(nc.scalar.copy, w_woven[2][:, i * P : (i + 1) * P, :], w_late[:, :, i * P : (i + 1) * P])
        quantize(nc, w_codes[2][:], w_scales[2][:], w_woven[2][:])
        windows.append(sb.tile([P, U], F32, name="window_last", tag="w_woven2", align_bytes=64))
        nc.gpsimd.memset(windows[GROUPS - 1][:], 0.0)
        for g in range(2):
            y = sb.tile([P, 2 * P], F32, name="y%d2" % g, tag="late" if g == 0 else "y12")
            product(g, [2], y[:], "turned1%d" % g, nc.scalar.copy)
            scatter(g, y[:], pieces[2])
        for g in range(2, GROUPS):
            y = sb.tile([P, S], F32, name="y%d" % g, align_bytes=64)
            product(g, [0, 1, 2], y[:], "turned0%d" % (g - 2), nc.scalar.copy)
            scatter(g, y[:], slice(0, S))

        codes_early = sb.tile([P, GROUPS - 1, QUARTER], U32, name="codes_early", tag="y3", align_bytes=64)
        scales_early = sb.tile([P, GROUPS - 1, QUARTER], U8, name="scales_early", align_bytes=64)
        codes_last = sb.tile([P, QUARTER], U32, name="codes_last", align_bytes=64)
        scales_last = sb.tile([P, QUARTER], U8, name="scales_last", align_bytes=64)

        for g in range(GROUPS):
            last = g == GROUPS - 1
            nc.sync.dma_start(out_0[g * P : (g + 1) * P, :], windows[g][:])
            regrouped = sb.tile([P, QUARTER, PACK], BF16, name="regrouped%d" % g, align_bytes=64)
            pairs = []
            for h in range(2):
                pair = ring.tile([P, 2, P, 2], BF16, name="pair")
                if last and h == 1:
                    parts = [(range(0, 2), "back00", nc.vector.tensor_copy), (range(2, 4), "back01", nc.scalar.copy)]
                else:
                    parts = [(range(4), "turned01" if last else "turned%d%d" % (g % 2, h), nc.scalar.copy)]
                for blocks, bank, copy in parts:
                    turned = ps.tile([P, len(blocks), P], F32, name="turned", tag=bank)
                    for i, q in enumerate(blocks):
                        c0 = q * QUARTER + h * P
                        nc.tensor.transpose(turned[:, i, :], windows[g][:, c0 : c0 + P], ident[:])
                    copy(
                        pair[:, :, 32 * blocks.start : 32 * blocks.stop, :],
                        turned[:].rearrange("c q (l u e) -> c u (q l) e", u=2, e=2),
                    )
                pairs.append(pair)
            for h in range(2):
                pair_words = pairs[h][:].rearrange("c u m e -> c (u m e)").bitcast(F32)
                back = ps.tile([P, 2, P], F32, name="back", tag="back%d%d" % (g % 2, h))
                for u in range(2):
                    nc.tensor.transpose(back[:, u, :], pair_words[:, u * P : (u + 1) * P], ident[:])
                cols = slice(h * P, (h + 1) * P)
                target = regrouped[:, cols, :].rearrange("m c t -> m (c t)").bitcast(F32)
                nc.scalar.copy(target.rearrange("m (c u) -> m c u", u=2), back[:].rearrange("m u c -> m c u"))
                if last:
                    quantize(nc, codes_last[:, cols], scales_last[:, cols], regrouped[:, cols, :])
            if not last:
                quantize(nc, codes_early[:, g, :], scales_early[:, g, :], regrouped[:])
            if g == GROUPS - 2:
                for q in range(4):
                    nc.sync.dma_start(scales_hbm[q, :, 0 : g + 1, :], scales_early[32 * q : 32 * q + 4].bitcast(I32))
                for q in range(4):
                    nc.sync.dma_start(words_hbm[q, :, 0 : g + 1, :], codes_early[32 * q : 32 * q + 32].bitcast(I32))

        for q in range(4):
            queue = nc.sync if q % 2 == 0 else nc.scalar
            queue.dma_start(words_hbm[q, :, GROUPS - 1, :], codes_last[32 * q : 32 * q + 32, :].bitcast(I32))
        for q in range(4):
            queue = nc.sync if q % 2 == 0 else nc.scalar
            queue.dma_start(scales_hbm[q, :, GROUPS - 1, :], scales_last[32 * q : 32 * q + 4, :].bitcast(I32))
